import numpy as np
import ml_dtypes


def mxq(x, axis, fmt="e4m3"):
    dtype, down = {"e4m3": (ml_dtypes.float8_e4m3fn, 7), "e5m2": (ml_dtypes.float8_e5m2, 14)}[fmt]
    v = np.moveaxis(np.asarray(x, np.float32).astype(ml_dtypes.bfloat16).astype(np.float64), axis, -1)
    blocks = v.reshape(v.shape[:-1] + (-1, 32))
    amax = np.abs(blocks).max(-1, keepdims=True)
    byte = np.maximum(np.where(amax > 0, np.frexp(amax)[1] - 1 + 127, 0) - down, 1)
    scale = np.exp2(byte - 127.0)
    codes = (blocks / scale).astype(np.float32).astype(dtype).astype(np.float64)
    return np.moveaxis((codes * scale).reshape(v.shape), -1, axis)


WIDE = False


def mx_kscale(k):
    if not WIDE:
        return np.ones(k)
    levels = np.array([10, -10, 5, -5, 0])
    if k % 512:
        return np.exp2(np.random.permutation(np.resize(levels, k // 32))).repeat(32)
    a = np.empty((k // 512, 16))
    for p in range(k // 512):
        a[p, :8] = np.random.permutation(np.resize(levels, 8))
        for g in range(8):
            far = levels[np.abs(levels - a[p, g]) >= 10]
            a[p, g + 8] = far[np.random.randint(len(far))]
    return np.exp2(a.ravel()).repeat(32)


def f64(x):
    return np.asarray(x).astype(np.float64)


def striped8(idx):
    return np.asarray(idx).reshape(8, -1, 16).transpose(0, 2, 1).reshape(128, -1).astype(np.uint16)


def unstriped8(offs):
    return offs.reshape(8, 16, -1).transpose(0, 2, 1).reshape(8, -1).astype(np.int64)


def pick8(x, idx, run):
    r = np.arange(len(x))
    return x[r[:, None], idx[r % (8 * run) // run]]


E2M1 = np.array([0.0, 0.5, 1.0, 1.5, 2.0, 3.0, 4.0, 6.0, -0.0, -0.5, -1.0, -1.5, -2.0, -3.0, -4.0, -6.0])


def pack_weight(w, fmt):
    k, n = w.shape
    w = f64(np.asarray(w, np.float32).astype(ml_dtypes.bfloat16)).reshape(k // 32, 32, n)
    amax = np.abs(w).max(1)
    if fmt == "e4m3":
        byte = np.frexp(amax)[1] - 1 + 127 - 7
    else:
        mant, ex = np.frexp(amax / 6.0)
        byte = np.where(mant > 0.5, ex, ex - 1) + 127
    byte = np.clip(np.where(amax > 0, byte, 1), 1, 254)
    scaled = (w * np.exp2(127.0 - byte)[:, None, :]).reshape(k, n).astype(np.float32)
    by_word = np.ascontiguousarray(scaled.reshape(k // 512, 128, 4, n).transpose(0, 1, 3, 2))
    if fmt == "e4m3":
        words = by_word.astype(ml_dtypes.float8_e4m3fn).view(np.uint8)
    else:
        c = by_word.astype(ml_dtypes.float4_e2m1fn).view(np.uint8) & 0xF
        words = (c[..., 0::2] | (c[..., 1::2] << 4)).reshape(k // 512, 128, 2 * n)
    return np.ascontiguousarray(words), np.ascontiguousarray(byte.astype(np.uint8).reshape(k // 512, 16, n))


def unpack_weight(words, scales, fmt):
    g, _, n = scales.shape
    words = np.ascontiguousarray(words).reshape(g, 128, n, -1)
    if fmt == "e4m3":
        vals = words.view(ml_dtypes.float8_e4m3fn).astype(np.float64)
    else:
        nib = np.empty((g, 128, n, 4), np.uint8)
        nib[..., 0::2] = words & 0xF
        nib[..., 1::2] = words >> 4
        vals = E2M1[nib]
    vals = vals * np.repeat(np.exp2(scales.astype(np.float64) - 127.0), 8, axis=1)[..., None]
    return vals.transpose(0, 1, 3, 2).reshape(g * 512, n)


D, K, T, U, I, Q = 512, 512, 1024, 1024, 512, 128


def setup_inputs():
    n = np.random.standard_normal
    idx = np.stack([np.random.permutation(T)[:I] for _ in range(8)])
    idx2 = np.stack([np.random.permutation(U)[:I] for _ in range(8)])
    idx3 = np.stack([np.random.permutation(T)[:I] for _ in range(8)])
    idx4 = np.stack([np.random.permutation(U)[:I] for _ in range(8)])
    idx5 = np.stack([np.random.permutation(T)[:I] for _ in range(8)])
    fd = mx_kscale(D)
    fk = mx_kscale(K)
    wqp = pack_weight(n((D, K)) * 1.0 / np.sqrt(D) * fd[:, None] * fk, "e4m3")
    cachep = pack_weight(n((K, T)) * 1.0 / np.sqrt(K) / fk[:, None], "e4m3")
    draftp = pack_weight(n((D, U)) * 1.0 / np.sqrt(D) * fd[:, None], "e2m1")
    return {
        "states": (n((D, Q)) * 0.95 / fd[:, None]).astype(np.float32),
        "wq_words": wqp[0],
        "wq_scales": wqp[1],
        "cache_words": cachep[0],
        "cache_scales": cachep[1],
        "draft_words": draftp[0],
        "draft_scales": draftp[1],
        "offs": striped8(idx),
        "offs2": striped8(idx2),
        "offs3": striped8(idx3),
        "offs4": striped8(idx4),
        "offs5": striped8(idx5),
    }


def reference(states, wq_words, wq_scales, cache_words, cache_scales, draft_words, draft_scales, offs, offs2, offs3, offs4, offs5):
    idx = unstriped8(offs)
    idx2 = unstriped8(offs2)
    idx3 = unstriped8(offs3)
    idx4 = unstriped8(offs4)
    idx5 = unstriped8(offs5)
    wqu = unpack_weight(wq_words, wq_scales, "e4m3")
    cacheu = unpack_weight(cache_words, cache_scales, "e4m3")
    draftu = unpack_weight(draft_words, draft_scales, "e2m1")
    statesq = mxq(f64(states), 0, "e4m3")
    qv = wqu.T @ statesq
    qvq = mxq(qv, 0, "e4m3")
    a = qvq.T @ cacheu
    b = statesq.T @ draftu
    f1 = np.zeros((Q, U))
    f1[np.arange(Q)[:, None], idx2[np.arange(Q) % 128 // 16]] = pick8(a, idx, 16)
    f2 = np.zeros((Q, T))
    f2[np.arange(Q)[:, None], idx[np.arange(Q) % 128 // 16]] = pick8(b, idx2, 16)
    aa = np.maximum(a, f2)
    bb = b - f1
    f3 = np.zeros((Q, T))
    f3[np.arange(Q)[:, None], idx3[np.arange(Q) % 128 // 16]] = pick8(bb, idx4, 16)
    ac = aa + f3
    y = pick8(ac, idx5, 16)
    return y

@@ -1,0 +1,160 @@
+from contextlib import ExitStack
+
+import concourse.mybir as mybir
+
+F32 = mybir.dt.float32
+BF16 = mybir.dt.bfloat16
+I32 = mybir.dt.int32
+U32 = mybir.dt.uint32
+U16 = mybir.dt.uint16
+U8 = mybir.dt.uint8
+FP8X4 = mybir.dt.float8_e4m3fn_x4
+FP4X4 = mybir.dt.float4_e2m1fn_x4
+COPY = mybir.ActivationFunctionType.Copy
+ALU = mybir.AluOpType
+
+P = 128
+D, K, T, U, SLOTS, Q = 512, 512, 1024, 1024, 512, 128
+HALF = SLOTS // 2
+PER_COLUMN = 16
+EARLY = 160
+A_PIECE = 256
+B_PIECE = 512
+
+FLOPS = 2 * Q * (D * K + K * T + D * U)
+
+
+def entries(offsets, first, last):
+    return offsets[:, first // PER_COLUMN : last // PER_COLUMN]
+
+
+def tile_attend_mutualput_side_kernel(tc, states, wq_words, wq_scales, cache_words, cache_scales, draft_words,
+                                       draft_scales, offs, offs2, offs3, offs4, offs5, out):
+    nc = tc.nc
+    with ExitStack() as ctx:
+        lists = ctx.enter_context(tc.tile_pool(name="lists", bufs=1))
+        sb = ctx.enter_context(tc.tile_pool(name="sb", bufs=1))
+        ps = ctx.enter_context(tc.psum_pool(name="ps", bufs=1))
+
+        def zeroed_plane(name, width):
+            plane = sb.tile([P, 4 * width], U8, name=name, align_bytes=64)
+            nc.vector.memset(plane[:, 0:width].bitcast(I32), 0)
+            return plane
+
+        def load_scale_rows(plane, scales):
+            nc.sync.dma_start(plane[0:4, :].bitcast(I32).rearrange("r (g n) -> r g n", g=4),
+                              scales[0].bitcast(I32).rearrange("(g r) n -> r g n", r=4))
+
+        def spread_scale_rows(plane, width):
+            for g in range(1, 4):
+                nc.vector.tensor_copy(plane[32 * g : 32 * g + 4, 0:width].bitcast(I32),
+                                      plane[0:4, g * width : (g + 1) * width].bitcast(I32))
+
+        wq_plane = zeroed_plane("wq_plane", K)
+        draft_plane = zeroed_plane("draft_plane", U)
+        cache_plane = zeroed_plane("cache_plane", T)
+
+        states_raw = sb.tile([P, 4, Q], F32)
+        nc.sync.dma_start(states_raw[:], states.rearrange("(p j) q -> p j q", j=4))
+        load_scale_rows(wq_plane, wq_scales)
+        wq_raw = sb.tile([P, K], I32)
+        nc.sync.dma_start(wq_raw[:], wq_words[0].rearrange("p n t -> p (n t)").bitcast(I32))
+        load_scale_rows(draft_plane, draft_scales)
+        draft_codes = sb.tile([P, 2 * U], U8, align_bytes=64)
+        nc.sync.dma_start(draft_codes[:].bitcast(I32), draft_words[0].bitcast(I32))
+        load_scale_rows(cache_plane, cache_scales)
+        cache_codes = sb.tile([P, T], I32, align_bytes=64)
+        nc.sync.dma_start(cache_codes[:], cache_words[0].rearrange("p n t -> p (n t)").bitcast(I32))
+        idx, idx2, idx3, idx4, idx5 = (lists.tile([P, SLOTS // PER_COLUMN], U16, name="idx%d" % n) for n in range(1, 6))
+        for tile, source in ((idx2, offs2), (idx, offs), (idx4, offs4), (idx3, offs3), (idx5, offs5)):
+            nc.sync.dma_start(tile[:], source)
+
+        f2 = sb.tile([P, T], F32)
+        nc.vector.memset(f2[:], 0.0)
+        f1 = sb.tile([P, U], F32)
+        nc.vector.memset(f1[:], 0.0)
+
+        states_bf = sb.tile([P, Q, 4], BF16, align_bytes=64)
+        nc.scalar.activation(states_bf[:].rearrange("p (c i) j -> p c j i", i=4),
+                             states_raw[:].rearrange("p j (c i) -> p c j i", i=4), COPY)
+        spread_scale_rows(wq_plane, K)
+        wq_dealt_scales = sb.tile([P, K], U8, align_bytes=64)
+        nc.vector.tensor_copy(wq_dealt_scales[:].rearrange("p (t c i) -> p c t i", t=4, i=16),
+                              wq_plane[:, 0:K].rearrange("p (c i t) -> p c t i", t=4, i=16))
+        states_codes = sb.tile([P, Q], U32, align_bytes=64)
+        states_scales = sb.tile([P, Q], U8, align_bytes=64)
+        nc.vector.quantize_mx(states_codes[:].bitcast(FP8X4), states_scales[:],
+                              states_bf[:].rearrange("p q j -> p (q j)"))
+        wq_low = sb.tile([P, 2 * P], U32, align_bytes=64)
+        wq_high = sb.tile([P, 2 * P], I32, align_bytes=64)
+        nc.scalar.copy(wq_low[:].rearrange("p (t c i) -> p c t i", t=2, i=4),
+                       wq_raw[:].bitcast(U32).rearrange("p (c i t) -> p c t i", t=4, i=4)[:, :, 0:2, :])
+        nc.vector.tensor_copy(wq_high[:].rearrange("p (t c i) -> p c t i", t=2, i=4),
+                              wq_raw[:].rearrange("p (c i t) -> p c t i", t=4, i=4)[:, :, 2:4, :])
+
+        qv_ps = ps.tile([P, 4, Q], F32)
+        for t in range(4):
+            half = wq_low if t < 2 else wq_high
+            nc.tensor.matmul_mx(qv_ps[:, t, :], lhsT=half[:, (t % 2) * P : (t % 2 + 1) * P].bitcast(FP8X4),
+                                lhsT_scale=wq_dealt_scales[:, t * P : (t + 1) * P],
+                                rhs=states_codes[:].bitcast(FP8X4), rhs_scale=states_scales[:], start=True, stop=True)
+        qv_bf = sb.tile([P, Q, 4], BF16, align_bytes=64, tag="qv_then_f3")
+        nc.scalar.copy(qv_bf[:], qv_ps[:].rearrange("p t q -> p q t"))
+
+        spread_scale_rows(draft_plane, U)
+        spread_scale_rows(cache_plane, T)
+
+        qv_codes = sb.tile([P, Q], U32, align_bytes=64)
+        qv_scales = sb.tile([P, Q], U8, align_bytes=64)
+        nc.vector.quantize_mx(qv_codes[:].bitcast(FP8X4), qv_scales[:], qv_bf[:].rearrange("p q t -> p (q t)"))
+
+        b = sb.tile([P, U], F32)
+        for first in range(0, U, B_PIECE):
+            b_ps = ps.tile([P, B_PIECE], F32, name="b_ps%d" % first)
+            nc.tensor.matmul_mx(b_ps[:], lhsT=states_codes[:].bitcast(FP8X4), lhsT_scale=states_scales[:],
+                                rhs=draft_codes[:, 2 * first : 2 * (first + B_PIECE)].bitcast(FP4X4),
+                                rhs_scale=draft_plane[:, first : first + B_PIECE], start=True, stop=True)
+            nc.scalar.copy(b[:, first : first + B_PIECE], b_ps[:])
+
+        a = sb.tile([P, T], F32)
+        for first in range(0, T, A_PIECE):
+            a_ps = ps.tile([P, A_PIECE], F32, name="a_ps%d" % first)
+            nc.tensor.matmul_mx(a_ps[:], lhsT=qv_codes[:].bitcast(FP8X4), lhsT_scale=qv_scales[:],
+                                rhs=cache_codes[:, first : first + A_PIECE].bitcast(FP8X4),
+                                rhs_scale=cache_plane[:, first : first + A_PIECE], start=True, stop=True)
+            nc.vector.tensor_copy(a[:, first : first + A_PIECE], a_ps[:])
+
+        f3 = sb.tile([P, T], F32, align_bytes=64, tag="qv_then_f3")
+        nc.vector.memset(f3[:], 0.0)
+
+        picked = sb.tile([P, SLOTS], F32)
+        a_late = sb.tile([P, HALF], F32)
+        nc.scalar.activation(picked[:, 0:HALF], b[:].indirect(entries(idx2, 0, HALF)), COPY)
+        nc.scalar.activation(f2[:].indirect(entries(idx, 0, EARLY)), picked[:, 0:EARLY], COPY)
+
+        nc.vector.tensor_copy(picked[:, HALF:SLOTS], a[:].indirect(entries(idx, 0, HALF)))
+        nc.vector.tensor_copy(a_late[:], a[:].indirect(entries(idx, HALF, SLOTS)))
+        nc.scalar.activation(f1[:].indirect(entries(idx2, 0, HALF)), picked[:, HALF:SLOTS], COPY)
+        nc.scalar.activation(f1[:].indirect(entries(idx2, HALF, SLOTS)), a_late[:], COPY)
+
+        nc.vector.tensor_copy(picked[:, HALF:SLOTS], b[:].indirect(entries(idx2, HALF, SLOTS)))
+        nc.scalar.activation(f2[:].indirect(entries(idx, EARLY, SLOTS)), picked[:, EARLY:SLOTS], COPY)
+
+        bb = sb.tile([P, U], F32, tag="bb_then_aa")
+        nc.vector.tensor_tensor(bb[:], b[:], f1[:], ALU.subtract)
+        for first in (0, HALF):
+            bb_picked = sb.tile([P, HALF], F32, name="bb_picked%d" % first)
+            nc.vector.tensor_copy(bb_picked[:], bb[:].indirect(entries(idx4, first, first + HALF)))
+            nc.scalar.activation(f3[:].indirect(entries(idx3, first, first + HALF)), bb_picked[:], COPY)
+
+        aa = sb.tile([P, T], F32, tag="bb_then_aa")
+        nc.vector.tensor_tensor(aa[:], a[:], f2[:], ALU.max)
+        ac = sb.tile([P, T], F32)
+        nc.vector.tensor_tensor(ac[:], aa[:], f3[:], ALU.add)
+
+        out_low = sb.tile([P, HALF], F32)
+        nc.vector.tensor_copy(out_low[:], ac[:].indirect(entries(idx5, 0, HALF)))
+        nc.sync.dma_start(out[:, 0:HALF], out_low[:])
+        out_high = sb.tile([P, HALF], F32)
+        nc.scalar.activation(out_high[:], ac[:].indirect(entries(idx5, HALF, SLOTS)), COPY)
+        nc.scalar.dma_start(out[:, HALF:SLOTS], out_high[:])

@@ -19,7 +19,8 @@ HALF = SLOTS // 2
 PER_COLUMN = 16
 EARLY = 160
 A_PIECE = 256
-B_PIECE = 512
+B_PIECE = 256
+FIRST = 192
 
 FLOPS = 2 * Q * (D * K + K * T + D * U)
 
@@ -37,50 +38,55 @@ def tile_attend_mutualput_side_kernel(tc, states, wq_words, wq_scales, cache_wor
         ps = ctx.enter_context(tc.psum_pool(name="ps", bufs=1))
 
         def zeroed_plane(name, width):
-            plane = sb.tile([P, 4 * width], U8, name=name, align_bytes=64)
-            nc.vector.memset(plane[:, 0:width].bitcast(I32), 0)
+            plane = sb.tile([P, width], U8, name=name, align_bytes=64)
+            nc.vector.memset(plane[:].bitcast(I32), 0)
             return plane
 
-        def load_scale_rows(plane, scales):
-            nc.sync.dma_start(plane[0:4, :].bitcast(I32).rearrange("r (g n) -> r g n", g=4),
-                              scales[0].bitcast(I32).rearrange("(g r) n -> r g n", r=4))
+        def load_scale_rows(tag, scales, width):
+            rows = sb.tile([4, 4, width // 4], I32, name="rows", tag=tag, align_bytes=64)
+            nc.sync.dma_start(rows[:], scales[0].bitcast(I32).rearrange("(g r) n -> r g n", r=4))
+            return rows
 
-        def spread_scale_rows(plane, width):
-            for g in range(1, 4):
-                nc.vector.tensor_copy(plane[32 * g : 32 * g + 4, 0:width].bitcast(I32),
-                                      plane[0:4, g * width : (g + 1) * width].bitcast(I32))
+        def spread_scale_rows(plane, rows):
+            for g in range(4):
+                nc.vector.tensor_copy(plane[32 * g : 32 * g + 4, :].bitcast(I32), rows[:, g, :])
+
+        def load_plane(plane, scales):
+            for g in range(4):
+                nc.sync.dma_start(plane[32 * g : 32 * g + 4, :].bitcast(I32),
+                                  scales[0, 4 * g : 4 * g + 4, :].bitcast(I32))
 
         wq_plane = zeroed_plane("wq_plane", K)
         draft_plane = zeroed_plane("draft_plane", U)
         cache_plane = zeroed_plane("cache_plane", T)
 
+        wq_rows = load_scale_rows("wq_rows", wq_scales, K)
         states_raw = sb.tile([P, 4, Q], F32)
         nc.sync.dma_start(states_raw[:], states.rearrange("(p j) q -> p j q", j=4))
-        load_scale_rows(wq_plane, wq_scales)
-        wq_raw = sb.tile([P, K], I32)
+        wq_raw = sb.tile([P, K], I32, tag="wq_then_f1")
         nc.sync.dma_start(wq_raw[:], wq_words[0].rearrange("p n t -> p (n t)").bitcast(I32))
-        load_scale_rows(draft_plane, draft_scales)
+        load_plane(draft_plane, draft_scales)
         draft_codes = sb.tile([P, 2 * U], U8, align_bytes=64)
         nc.sync.dma_start(draft_codes[:].bitcast(I32), draft_words[0].bitcast(I32))
-        load_scale_rows(cache_plane, cache_scales)
-        cache_codes = sb.tile([P, T], I32, align_bytes=64)
+        cache_codes = sb.tile([P, T], I32, align_bytes=64, tag="cache_then_f3")
         nc.sync.dma_start(cache_codes[:], cache_words[0].rearrange("p n t -> p (n t)").bitcast(I32))
+        load_plane(cache_plane, cache_scales)
         idx, idx2, idx3, idx4, idx5 = (lists.tile([P, SLOTS // PER_COLUMN], U16, name="idx%d" % n) for n in range(1, 6))
         for tile, source in ((idx2, offs2), (idx, offs), (idx4, offs4), (idx3, offs3), (idx5, offs5)):
             nc.sync.dma_start(tile[:], source)
 
         f2 = sb.tile([P, T], F32)
         nc.vector.memset(f2[:], 0.0)
-        f1 = sb.tile([P, U], F32)
-        nc.vector.memset(f1[:], 0.0)
+        f1_first = sb.tile([P, U], F32)
+        nc.vector.memset(f1_first[:], 0.0)
 
         states_bf = sb.tile([P, Q, 4], BF16, align_bytes=64)
         nc.scalar.activation(states_bf[:].rearrange("p (c i) j -> p c j i", i=4),
                              states_raw[:].rearrange("p j (c i) -> p c j i", i=4), COPY)
-        spread_scale_rows(wq_plane, K)
+        spread_scale_rows(wq_plane, wq_rows)
         wq_dealt_scales = sb.tile([P, K], U8, align_bytes=64)
         nc.vector.tensor_copy(wq_dealt_scales[:].rearrange("p (t c i) -> p c t i", t=4, i=16),
-                              wq_plane[:, 0:K].rearrange("p (c i t) -> p c t i", t=4, i=16))
+                              wq_plane[:].rearrange("p (c i t) -> p c t i", t=4, i=16))
         states_codes = sb.tile([P, Q], U32, align_bytes=64)
         states_scales = sb.tile([P, Q], U8, align_bytes=64)
         nc.vector.quantize_mx(states_codes[:].bitcast(FP8X4), states_scales[:],
@@ -92,17 +98,18 @@ def tile_attend_mutualput_side_kernel(tc, states, wq_words, wq_scales, cache_wor
         nc.vector.tensor_copy(wq_high[:].rearrange("p (t c i) -> p c t i", t=2, i=4),
                               wq_raw[:].rearrange("p (c i t) -> p c t i", t=4, i=4)[:, :, 2:4, :])
 
-        qv_ps = ps.tile([P, 4, Q], F32)
+        f1_rest = sb.tile([P, U], F32, tag="wq_then_f1")
+        nc.gpsimd.memset(f1_rest[:], 0.0)
+
+        qv_ps = ps.tile([P, 4, Q], F32, tag="qv_then_a")
         for t in range(4):
             half = wq_low if t < 2 else wq_high
             nc.tensor.matmul_mx(qv_ps[:, t, :], lhsT=half[:, (t % 2) * P : (t % 2 + 1) * P].bitcast(FP8X4),
                                 lhsT_scale=wq_dealt_scales[:, t * P : (t + 1) * P],
                                 rhs=states_codes[:].bitcast(FP8X4), rhs_scale=states_scales[:], start=True, stop=True)
         qv_bf = sb.tile([P, Q, 4], BF16, align_bytes=64, tag="qv_then_f3")
-        nc.scalar.copy(qv_bf[:], qv_ps[:].rearrange("p t q -> p q t"))
+        nc.vector.tensor_copy(qv_bf[:], qv_ps[:].rearrange("p t q -> p q t"))
 
-        spread_scale_rows(draft_plane, U)
-        spread_scale_rows(cache_plane, T)
 
         qv_codes = sb.tile([P, Q], U32, align_bytes=64)
         qv_scales = sb.tile([P, Q], U8, align_bytes=64)
@@ -118,39 +125,48 @@ def tile_attend_mutualput_side_kernel(tc, states, wq_words, wq_scales, cache_wor
 
         a = sb.tile([P, T], F32)
         for first in range(0, T, A_PIECE):
-            a_ps = ps.tile([P, A_PIECE], F32, name="a_ps%d" % first)
+            a_ps = ps.tile([P, A_PIECE], F32, name="a_ps", tag="qv_then_a" if first + A_PIECE == T else "a_ps%d" % first)
             nc.tensor.matmul_mx(a_ps[:], lhsT=qv_codes[:].bitcast(FP8X4), lhsT_scale=qv_scales[:],
                                 rhs=cache_codes[:, first : first + A_PIECE].bitcast(FP8X4),
                                 rhs_scale=cache_plane[:, first : first + A_PIECE], start=True, stop=True)
             nc.vector.tensor_copy(a[:, first : first + A_PIECE], a_ps[:])
 
-        f3 = sb.tile([P, T], F32, align_bytes=64, tag="qv_then_f3")
-        nc.vector.memset(f3[:], 0.0)
+        f3_first = sb.tile([P, T], F32, align_bytes=64, tag="qv_then_f3")
+        nc.gpsimd.memset(f3_first[:], 0.0)
+        f3_rest = sb.tile([P, T], F32, align_bytes=64, tag="cache_then_f3")
+        nc.gpsimd.memset(f3_rest[:], 0.0)
 
-        picked = sb.tile([P, SLOTS], F32)
-        a_late = sb.tile([P, HALF], F32)
-        nc.scalar.activation(picked[:, 0:HALF], b[:].indirect(entries(idx2, 0, HALF)), COPY)
-        nc.scalar.activation(f2[:].indirect(entries(idx, 0, EARLY)), picked[:, 0:EARLY], COPY)
+        picked = sb.tile([P, 2 * SLOTS - FIRST], F32)
+        b_picked = picked[:, 0:SLOTS]
+        a_picked = picked[:, SLOTS - FIRST : 2 * SLOTS - FIRST]
+        nc.scalar.activation(b_picked[:, 0:HALF], b[:].indirect(entries(idx2, 0, HALF)), COPY)
+        nc.scalar.activation(f2[:].indirect(entries(idx, 0, EARLY)), b_picked[:, 0:EARLY], COPY)
 
-        nc.vector.tensor_copy(picked[:, HALF:SLOTS], a[:].indirect(entries(idx, 0, HALF)))
-        nc.vector.tensor_copy(a_late[:], a[:].indirect(entries(idx, HALF, SLOTS)))
-        nc.scalar.activation(f1[:].indirect(entries(idx2, 0, HALF)), picked[:, HALF:SLOTS], COPY)
-        nc.scalar.activation(f1[:].indirect(entries(idx2, HALF, SLOTS)), a_late[:], COPY)
-
-        nc.vector.tensor_copy(picked[:, HALF:SLOTS], b[:].indirect(entries(idx2, HALF, SLOTS)))
-        nc.scalar.activation(f2[:].indirect(entries(idx, EARLY, SLOTS)), picked[:, EARLY:SLOTS], COPY)
-
-        bb = sb.tile([P, U], F32, tag="bb_then_aa")
-        nc.vector.tensor_tensor(bb[:], b[:], f1[:], ALU.subtract)
         for first in (0, HALF):
-            bb_picked = sb.tile([P, HALF], F32, name="bb_picked%d" % first)
-            nc.vector.tensor_copy(bb_picked[:], bb[:].indirect(entries(idx4, first, first + HALF)))
-            nc.scalar.activation(f3[:].indirect(entries(idx3, first, first + HALF)), bb_picked[:], COPY)
+            nc.vector.tensor_copy(a_picked[:, first : first + HALF], a[:].indirect(entries(idx, first, first + HALF)))
+        nc.scalar.activation(f1_first[:].indirect(entries(idx2, 0, FIRST)), a_picked[:, 0:FIRST], COPY)
+        nc.scalar.activation(f1_rest[:].indirect(entries(idx2, FIRST, SLOTS)), a_picked[:, FIRST:SLOTS], COPY)
+
+        nc.vector.tensor_copy(b_picked[:, HALF:SLOTS], b[:].indirect(entries(idx2, HALF, SLOTS)))
+        nc.scalar.activation(f2[:].indirect(entries(idx, EARLY, SLOTS)), b_picked[:, EARLY:SLOTS], COPY)
+
+        bb_part = sb.tile([P, U], F32)
+        nc.vector.tensor_tensor(bb_part[:], b[:], f1_first[:], ALU.subtract)
+        bb = sb.tile([P, U], F32, tag="bb_then_aa")
+        nc.vector.tensor_tensor(bb[:], bb_part[:], f1_rest[:], ALU.subtract)
+        bb_picked = sb.tile([P, SLOTS], F32)
+        for first in (0, HALF):
+            nc.vector.tensor_copy(bb_picked[:, first : first + HALF],
+                                  bb[:].indirect(entries(idx4, first, first + HALF)))
+        nc.scalar.activation(f3_first[:].indirect(entries(idx3, 0, FIRST)), bb_picked[:, 0:FIRST], COPY)
+        nc.scalar.activation(f3_rest[:].indirect(entries(idx3, FIRST, SLOTS)), bb_picked[:, FIRST:SLOTS], COPY)
 
         aa = sb.tile([P, T], F32, tag="bb_then_aa")
         nc.vector.tensor_tensor(aa[:], a[:], f2[:], ALU.max)
+        ac_part = sb.tile([P, T], F32)
+        nc.vector.tensor_tensor(ac_part[:], aa[:], f3_first[:], ALU.add)
         ac = sb.tile([P, T], F32)
-        nc.vector.tensor_tensor(ac[:], aa[:], f3[:], ALU.add)
+        nc.vector.tensor_tensor(ac[:], ac_part[:], f3_rest[:], ALU.add)
 
         out_low = sb.tile([P, HALF], F32)
         nc.vector.tensor_copy(out_low[:], ac[:].indirect(entries(idx5, 0, HALF)))

@@ -17,7 +17,7 @@ P = 128
 D, K, T, U, SLOTS, Q = 512, 512, 1024, 1024, 512, 128
 HALF = SLOTS // 2
 PER_COLUMN = 16
-EARLY = 160
+EARLY = 96
 A_PIECE = 256
 B_PIECE = 256
 FIRST = 192
@@ -42,15 +42,6 @@ def tile_attend_mutualput_side_kernel(tc, states, wq_words, wq_scales, cache_wor
             nc.vector.memset(plane[:].bitcast(I32), 0)
             return plane
 
-        def load_scale_rows(tag, scales, width):
-            rows = sb.tile([4, 4, width // 4], I32, name="rows", tag=tag, align_bytes=64)
-            nc.sync.dma_start(rows[:], scales[0].bitcast(I32).rearrange("(g r) n -> r g n", r=4))
-            return rows
-
-        def spread_scale_rows(plane, rows):
-            for g in range(4):
-                nc.vector.tensor_copy(plane[32 * g : 32 * g + 4, :].bitcast(I32), rows[:, g, :])
-
         def load_plane(plane, scales):
             for g in range(4):
                 nc.sync.dma_start(plane[32 * g : 32 * g + 4, :].bitcast(I32),
@@ -60,7 +51,10 @@ def tile_attend_mutualput_side_kernel(tc, states, wq_words, wq_scales, cache_wor
         draft_plane = zeroed_plane("draft_plane", U)
         cache_plane = zeroed_plane("cache_plane", T)
 
-        wq_rows = load_scale_rows("wq_rows", wq_scales, K)
+        wq_rows = sb.tile([P, 2, K // 4], I32)
+        for pair in range(2):
+            nc.sync.dma_start(wq_rows[64 * pair : 64 * pair + 4],
+                              wq_scales[0, 8 * pair : 8 * pair + 8, :].bitcast(I32).rearrange("(g r) n -> r g n", r=4))
         states_raw = sb.tile([P, 4, Q], F32)
         nc.sync.dma_start(states_raw[:], states.rearrange("(p j) q -> p j q", j=4))
         wq_raw = sb.tile([P, K], I32, tag="wq_then_f1")
@@ -83,7 +77,9 @@ def tile_attend_mutualput_side_kernel(tc, states, wq_words, wq_scales, cache_wor
         states_bf = sb.tile([P, Q, 4], BF16, align_bytes=64)
         nc.scalar.activation(states_bf[:].rearrange("p (c i) j -> p c j i", i=4),
                              states_raw[:].rearrange("p j (c i) -> p c j i", i=4), COPY)
-        spread_scale_rows(wq_plane, wq_rows)
+        for g in range(4):
+            nc.vector.tensor_copy(wq_plane[32 * g : 32 * g + 4, :].bitcast(I32),
+                                  wq_rows[64 * (g // 2) : 64 * (g // 2) + 4, g % 2, :])
         wq_dealt_scales = sb.tile([P, K], U8, align_bytes=64)
         nc.vector.tensor_copy(wq_dealt_scales[:].rearrange("p (t c i) -> p c t i", t=4, i=16),
                               wq_plane[:].rearrange("p (c i t) -> p c t i", t=4, i=16))
@@ -101,17 +97,22 @@ def tile_attend_mutualput_side_kernel(tc, states, wq_words, wq_scales, cache_wor
         f1_rest = sb.tile([P, U], F32, tag="wq_then_f1")
         nc.gpsimd.memset(f1_rest[:], 0.0)
 
-        qv_ps = ps.tile([P, 4, Q], F32, tag="qv_then_a")
-        for t in range(4):
-            half = wq_low if t < 2 else wq_high
-            nc.tensor.matmul_mx(qv_ps[:, t, :], lhsT=half[:, (t % 2) * P : (t % 2 + 1) * P].bitcast(FP8X4),
-                                lhsT_scale=wq_dealt_scales[:, t * P : (t + 1) * P],
-                                rhs=states_codes[:].bitcast(FP8X4), rhs_scale=states_scales[:], start=True, stop=True)
         qv_bf = sb.tile([P, Q, 4], BF16, align_bytes=64, tag="qv_then_f3")
-        nc.vector.tensor_copy(qv_bf[:], qv_ps[:].rearrange("p t q -> p q t"))
+        for pair, wq_pair in enumerate((wq_low, wq_high)):
+            qv_ps = ps.tile([P, 2, Q], F32, name="qv_ps", tag="qv_then_a%d" % pair)
+            for e in range(2):
+                t = 2 * pair + e
+                nc.tensor.matmul_mx(qv_ps[:, e, :], lhsT=wq_pair[:, e * P : (e + 1) * P].bitcast(FP8X4),
+                                    lhsT_scale=wq_dealt_scales[:, t * P : (t + 1) * P],
+                                    rhs=states_codes[:].bitcast(FP8X4), rhs_scale=states_scales[:],
+                                    start=True, stop=True)
+            words = qv_bf[:, :, 2 * pair : 2 * pair + 2]
+            if pair == 0:
+                nc.scalar.copy(words, qv_ps[:].rearrange("p e q -> p q e"))
+            else:
+                nc.vector.tensor_copy(words, qv_ps[:].rearrange("p e q -> p q e"))
 
-
-        qv_codes = sb.tile([P, Q], U32, align_bytes=64)
+        qv_codes = sb.tile([P, Q], U32, align_bytes=64, tag="qv_codes_then_picked")
         qv_scales = sb.tile([P, Q], U8, align_bytes=64)
         nc.vector.quantize_mx(qv_codes[:].bitcast(FP8X4), qv_scales[:], qv_bf[:].rearrange("p q t -> p (q t)"))
 
@@ -125,21 +126,24 @@ def tile_attend_mutualput_side_kernel(tc, states, wq_words, wq_scales, cache_wor
 
         a = sb.tile([P, T], F32)
         for first in range(0, T, A_PIECE):
-            a_ps = ps.tile([P, A_PIECE], F32, name="a_ps", tag="qv_then_a" if first + A_PIECE == T else "a_ps%d" % first)
+            a_ps = ps.tile([P, A_PIECE], F32, name="a_ps", tag="qv_then_a%d" % (first // A_PIECE - 2) if first >= T // 2 else "a_ps%d" % first)
             nc.tensor.matmul_mx(a_ps[:], lhsT=qv_codes[:].bitcast(FP8X4), lhsT_scale=qv_scales[:],
                                 rhs=cache_codes[:, first : first + A_PIECE].bitcast(FP8X4),
                                 rhs_scale=cache_plane[:, first : first + A_PIECE], start=True, stop=True)
-            nc.vector.tensor_copy(a[:, first : first + A_PIECE], a_ps[:])
+            if first < T // 2:
+                nc.vector.tensor_copy(a[:, first : first + A_PIECE], a_ps[:])
+            else:
+                nc.scalar.copy(a[:, first : first + A_PIECE], a_ps[:])
 
         f3_first = sb.tile([P, T], F32, align_bytes=64, tag="qv_then_f3")
         nc.gpsimd.memset(f3_first[:], 0.0)
         f3_rest = sb.tile([P, T], F32, align_bytes=64, tag="cache_then_f3")
         nc.gpsimd.memset(f3_rest[:], 0.0)
 
-        picked = sb.tile([P, 2 * SLOTS - FIRST], F32)
+        picked = sb.tile([P, 2 * SLOTS - FIRST], F32, align_bytes=64, tag="qv_codes_then_picked")
         b_picked = picked[:, 0:SLOTS]
         a_picked = picked[:, SLOTS - FIRST : 2 * SLOTS - FIRST]
-        nc.scalar.activation(b_picked[:, 0:HALF], b[:].indirect(entries(idx2, 0, HALF)), COPY)
+        nc.vector.tensor_copy(b_picked[:, 0:HALF], b[:].indirect(entries(idx2, 0, HALF)))
         nc.scalar.activation(f2[:].indirect(entries(idx, 0, EARLY)), b_picked[:, 0:EARLY], COPY)
 
         for first in (0, HALF):

@@ -60,11 +60,17 @@ def tile_attend_mutualput_side_kernel(tc, states, wq_words, wq_scales, cache_wor
         wq_raw = sb.tile([P, K], I32, tag="wq_then_f1")
         nc.sync.dma_start(wq_raw[:], wq_words[0].rearrange("p n t -> p (n t)").bitcast(I32))
         load_plane(draft_plane, draft_scales)
-        draft_codes = sb.tile([P, 2 * U], U8, align_bytes=64)
-        nc.sync.dma_start(draft_codes[:].bitcast(I32), draft_words[0].bitcast(I32))
-        cache_codes = sb.tile([P, T], I32, align_bytes=64, tag="cache_then_f3")
-        nc.sync.dma_start(cache_codes[:], cache_words[0].rearrange("p n t -> p (n t)").bitcast(I32))
+        draft_halves = []
+        for half in range(2):
+            draft_half = sb.tile([P, U], U8, name="draft_half%d" % half, align_bytes=64)
+            nc.sync.dma_start(draft_half[:].bitcast(I32), draft_words[0][:, half * U : (half + 1) * U].bitcast(I32))
+            draft_halves.append(draft_half)
+        cache_all = cache_words[0].rearrange("p n t -> p (n t)").bitcast(I32)
+        cache_low = sb.tile([P, T // 2], I32, align_bytes=64)
+        nc.sync.dma_start(cache_low[:], cache_all[:, 0 : T // 2])
         load_plane(cache_plane, cache_scales)
+        cache_high = sb.tile([P, T // 2], I32, align_bytes=64)
+        nc.sync.dma_start(cache_high[:], cache_all[:, T // 2 : T])
         idx, idx2, idx3, idx4, idx5 = (lists.tile([P, SLOTS // PER_COLUMN], U16, name="idx%d" % n) for n in range(1, 6))
         for tile, source in ((idx2, offs2), (idx, offs), (idx4, offs4), (idx3, offs3), (idx5, offs5)):
             nc.sync.dma_start(tile[:], source)
@@ -116,19 +122,21 @@ def tile_attend_mutualput_side_kernel(tc, states, wq_words, wq_scales, cache_wor
         qv_scales = sb.tile([P, Q], U8, align_bytes=64)
         nc.vector.quantize_mx(qv_codes[:].bitcast(FP8X4), qv_scales[:], qv_bf[:].rearrange("p q t -> p (q t)"))
 
-        b = sb.tile([P, U], F32)
+        b = sb.tile([P, U], F32, tag="b_then_f3")
         for first in range(0, U, B_PIECE):
+            within = first % (U // 2)
             b_ps = ps.tile([P, B_PIECE], F32, name="b_ps%d" % first)
             nc.tensor.matmul_mx(b_ps[:], lhsT=states_codes[:].bitcast(FP8X4), lhsT_scale=states_scales[:],
-                                rhs=draft_codes[:, 2 * first : 2 * (first + B_PIECE)].bitcast(FP4X4),
+                                rhs=draft_halves[first // (U // 2)][:, 2 * within : 2 * (within + B_PIECE)].bitcast(FP4X4),
                                 rhs_scale=draft_plane[:, first : first + B_PIECE], start=True, stop=True)
             nc.scalar.copy(b[:, first : first + B_PIECE], b_ps[:])
 
         a = sb.tile([P, T], F32)
         for first in range(0, T, A_PIECE):
+            within = first % (T // 2)
             a_ps = ps.tile([P, A_PIECE], F32, name="a_ps", tag="qv_then_a%d" % (first // A_PIECE - 2) if first >= T // 2 else "a_ps%d" % first)
             nc.tensor.matmul_mx(a_ps[:], lhsT=qv_codes[:].bitcast(FP8X4), lhsT_scale=qv_scales[:],
-                                rhs=cache_codes[:, first : first + A_PIECE].bitcast(FP8X4),
+                                rhs=(cache_low, cache_high)[first // (T // 2)][:, within : within + A_PIECE].bitcast(FP8X4),
                                 rhs_scale=cache_plane[:, first : first + A_PIECE], start=True, stop=True)
             if first < T // 2:
                 nc.vector.tensor_copy(a[:, first : first + A_PIECE], a_ps[:])
@@ -137,8 +145,6 @@ def tile_attend_mutualput_side_kernel(tc, states, wq_words, wq_scales, cache_wor
 
         f3_first = sb.tile([P, T], F32, align_bytes=64, tag="qv_then_f3")
         nc.gpsimd.memset(f3_first[:], 0.0)
-        f3_rest = sb.tile([P, T], F32, align_bytes=64, tag="cache_then_f3")
-        nc.gpsimd.memset(f3_rest[:], 0.0)
 
         picked = sb.tile([P, 2 * SLOTS - FIRST], F32, align_bytes=64, tag="qv_codes_then_picked")
         b_picked = picked[:, 0:SLOTS]
@@ -156,6 +162,8 @@ def tile_attend_mutualput_side_kernel(tc, states, wq_words, wq_scales, cache_wor
 
         bb_part = sb.tile([P, U], F32)
         nc.vector.tensor_tensor(bb_part[:], b[:], f1_first[:], ALU.subtract)
+        f3_rest = sb.tile([P, T], F32, tag="b_then_f3")
+        nc.gpsimd.memset(f3_rest[:], 0.0)
         bb = sb.tile([P, U], F32, tag="bb_then_aa")
         nc.vector.tensor_tensor(bb[:], bb_part[:], f1_rest[:], ALU.subtract)
         bb_picked = sb.tile([P, SLOTS], F32)

from contextlib import ExitStack

import concourse.mybir as mybir

F32 = mybir.dt.float32
BF16 = mybir.dt.bfloat16
I32 = mybir.dt.int32
U32 = mybir.dt.uint32
U16 = mybir.dt.uint16
U8 = mybir.dt.uint8
FP8X4 = mybir.dt.float8_e4m3fn_x4
FP4X4 = mybir.dt.float4_e2m1fn_x4
COPY = mybir.ActivationFunctionType.Copy
ALU = mybir.AluOpType

P = 128
D, K, T, U, SLOTS, Q = 512, 512, 1024, 1024, 512, 128
HALF = SLOTS // 2
PER_COLUMN = 16
EARLY = 96
A_PIECE = 256
B_PIECE = 256
FIRST = 192

FLOPS = 2 * Q * (D * K + K * T + D * U)


def entries(offsets, first, last):
    return offsets[:, first // PER_COLUMN : last // PER_COLUMN]


def tile_attend_mutualput_side_kernel(tc, states, wq_words, wq_scales, cache_words, cache_scales, draft_words,
                                       draft_scales, offs, offs2, offs3, offs4, offs5, out):
    nc = tc.nc
    with ExitStack() as ctx:
        lists = ctx.enter_context(tc.tile_pool(name="lists", bufs=1))
        sb = ctx.enter_context(tc.tile_pool(name="sb", bufs=1))
        ps = ctx.enter_context(tc.psum_pool(name="ps", bufs=1))

        def zeroed_plane(name, width):
            plane = sb.tile([P, width], U8, name=name, align_bytes=64)
            nc.vector.memset(plane[:].bitcast(I32), 0)
            return plane

        def load_plane(plane, scales):
            for g in range(4):
                nc.sync.dma_start(plane[32 * g : 32 * g + 4, :].bitcast(I32),
                                  scales[0, 4 * g : 4 * g + 4, :].bitcast(I32))

        wq_plane = zeroed_plane("wq_plane", K)
        draft_plane = zeroed_plane("draft_plane", U)
        cache_plane = zeroed_plane("cache_plane", T)

        wq_rows = sb.tile([P, 2, K // 4], I32)
        for pair in range(2):
            nc.sync.dma_start(wq_rows[64 * pair : 64 * pair + 4],
                              wq_scales[0, 8 * pair : 8 * pair + 8, :].bitcast(I32).rearrange("(g r) n -> r g n", r=4))
        states_raw = sb.tile([P, 4, Q], F32)
        nc.sync.dma_start(states_raw[:], states.rearrange("(p j) q -> p j q", j=4))
        wq_raw = sb.tile([P, K], I32, tag="wq_then_f1")
        nc.sync.dma_start(wq_raw[:], wq_words[0].rearrange("p n t -> p (n t)").bitcast(I32))
        load_plane(draft_plane, draft_scales)
        draft_halves = []
        for half in range(2):
            draft_half = sb.tile([P, U], U8, name="draft_half%d" % half, align_bytes=64)
            nc.sync.dma_start(draft_half[:].bitcast(I32), draft_words[0][:, half * U : (half + 1) * U].bitcast(I32))
            draft_halves.append(draft_half)
        cache_all = cache_words[0].rearrange("p n t -> p (n t)").bitcast(I32)
        cache_low = sb.tile([P, T // 2], I32, align_bytes=64)
        nc.sync.dma_start(cache_low[:], cache_all[:, 0 : T // 2])
        load_plane(cache_plane, cache_scales)
        cache_high = sb.tile([P, T // 2], I32, align_bytes=64)
        nc.sync.dma_start(cache_high[:], cache_all[:, T // 2 : T])
        idx, idx2, idx3, idx4, idx5 = (lists.tile([P, SLOTS // PER_COLUMN], U16, name="idx%d" % n) for n in range(1, 6))
        for tile, source in ((idx2, offs2), (idx, offs), (idx4, offs4), (idx3, offs3), (idx5, offs5)):
            nc.sync.dma_start(tile[:], source)

        f2 = sb.tile([P, T], F32)
        nc.vector.memset(f2[:], 0.0)
        f1_first = sb.tile([P, U], F32)
        nc.vector.memset(f1_first[:], 0.0)

        states_bf = sb.tile([P, Q, 4], BF16, align_bytes=64)
        nc.scalar.activation(states_bf[:].rearrange("p (c i) j -> p c j i", i=4),
                             states_raw[:].rearrange("p j (c i) -> p c j i", i=4), COPY)
        for g in range(4):
            nc.vector.tensor_copy(wq_plane[32 * g : 32 * g + 4, :].bitcast(I32),
                                  wq_rows[64 * (g // 2) : 64 * (g // 2) + 4, g % 2, :])
        wq_dealt_scales = sb.tile([P, K], U8, align_bytes=64)
        nc.vector.tensor_copy(wq_dealt_scales[:].rearrange("p (t c i) -> p c t i", t=4, i=16),
                              wq_plane[:].rearrange("p (c i t) -> p c t i", t=4, i=16))
        states_codes = sb.tile([P, Q], U32, align_bytes=64)
        states_scales = sb.tile([P, Q], U8, align_bytes=64)
        nc.vector.quantize_mx(states_codes[:].bitcast(FP8X4), states_scales[:],
                              states_bf[:].rearrange("p q j -> p (q j)"))
        wq_low = sb.tile([P, 2 * P], U32, align_bytes=64)
        wq_high = sb.tile([P, 2 * P], I32, align_bytes=64)
        nc.scalar.copy(wq_low[:].rearrange("p (t c i) -> p c t i", t=2, i=4),
                       wq_raw[:].bitcast(U32).rearrange("p (c i t) -> p c t i", t=4, i=4)[:, :, 0:2, :])
        nc.vector.tensor_copy(wq_high[:].rearrange("p (t c i) -> p c t i", t=2, i=4),
                              wq_raw[:].rearrange("p (c i t) -> p c t i", t=4, i=4)[:, :, 2:4, :])

        f1_rest = sb.tile([P, U], F32, tag="wq_then_f1")
        nc.gpsimd.memset(f1_rest[:], 0.0)

        qv_bf = sb.tile([P, Q, 4], BF16, align_bytes=64, tag="qv_then_f3")
        for pair, wq_pair in enumerate((wq_low, wq_high)):
            qv_ps = ps.tile([P, 2, Q], F32, name="qv_ps", tag="qv_then_a%d" % pair)
            for e in range(2):
                t = 2 * pair + e
                nc.tensor.matmul_mx(qv_ps[:, e, :], lhsT=wq_pair[:, e * P : (e + 1) * P].bitcast(FP8X4),
                                    lhsT_scale=wq_dealt_scales[:, t * P : (t + 1) * P],
                                    rhs=states_codes[:].bitcast(FP8X4), rhs_scale=states_scales[:],
                                    start=True, stop=True)
            words = qv_bf[:, :, 2 * pair : 2 * pair + 2]
            if pair == 0:
                nc.scalar.copy(words, qv_ps[:].rearrange("p e q -> p q e"))
            else:
                nc.vector.tensor_copy(words, qv_ps[:].rearrange("p e q -> p q e"))

        qv_codes = sb.tile([P, Q], U32, align_bytes=64, tag="qv_codes_then_picked")
        qv_scales = sb.tile([P, Q], U8, align_bytes=64)
        nc.vector.quantize_mx(qv_codes[:].bitcast(FP8X4), qv_scales[:], qv_bf[:].rearrange("p q t -> p (q t)"))

        b = sb.tile([P, U], F32, tag="b_then_f3")
        for first in range(0, U, B_PIECE):
            within = first % (U // 2)
            b_ps = ps.tile([P, B_PIECE], F32, name="b_ps%d" % first)
            nc.tensor.matmul_mx(b_ps[:], lhsT=states_codes[:].bitcast(FP8X4), lhsT_scale=states_scales[:],
                                rhs=draft_halves[first // (U // 2)][:, 2 * within : 2 * (within + B_PIECE)].bitcast(FP4X4),
                                rhs_scale=draft_plane[:, first : first + B_PIECE], start=True, stop=True)
            nc.scalar.copy(b[:, first : first + B_PIECE], b_ps[:])

        a = sb.tile([P, T], F32)
        for first in range(0, T, A_PIECE):
            within = first % (T // 2)
            a_ps = ps.tile([P, A_PIECE], F32, name="a_ps", tag="qv_then_a%d" % (first // A_PIECE - 2) if first >= T // 2 else "a_ps%d" % first)
            nc.tensor.matmul_mx(a_ps[:], lhsT=qv_codes[:].bitcast(FP8X4), lhsT_scale=qv_scales[:],
                                rhs=(cache_low, cache_high)[first // (T // 2)][:, within : within + A_PIECE].bitcast(FP8X4),
                                rhs_scale=cache_plane[:, first : first + A_PIECE], start=True, stop=True)
            if first < T // 2:
                nc.vector.tensor_copy(a[:, first : first + A_PIECE], a_ps[:])
            else:
                nc.scalar.copy(a[:, first : first + A_PIECE], a_ps[:])

        f3_first = sb.tile([P, T], F32, align_bytes=64, tag="qv_then_f3")
        nc.gpsimd.memset(f3_first[:], 0.0)

        picked = sb.tile([P, 2 * SLOTS - FIRST], F32, align_bytes=64, tag="qv_codes_then_picked")
        b_picked = picked[:, 0:SLOTS]
        a_picked = picked[:, SLOTS - FIRST : 2 * SLOTS - FIRST]
        nc.vector.tensor_copy(b_picked[:, 0:HALF], b[:].indirect(entries(idx2, 0, HALF)))
        nc.scalar.activation(f2[:].indirect(entries(idx, 0, EARLY)), b_picked[:, 0:EARLY], COPY)

        for first in (0, HALF):
            nc.vector.tensor_copy(a_picked[:, first : first + HALF], a[:].indirect(entries(idx, first, first + HALF)))
        nc.scalar.activation(f1_first[:].indirect(entries(idx2, 0, FIRST)), a_picked[:, 0:FIRST], COPY)
        nc.scalar.activation(f1_rest[:].indirect(entries(idx2, FIRST, SLOTS)), a_picked[:, FIRST:SLOTS], COPY)

        nc.vector.tensor_copy(b_picked[:, HALF:SLOTS], b[:].indirect(entries(idx2, HALF, SLOTS)))
        nc.scalar.activation(f2[:].indirect(entries(idx, EARLY, SLOTS)), b_picked[:, EARLY:SLOTS], COPY)

        bb_part = sb.tile([P, U], F32)
        nc.vector.tensor_tensor(bb_part[:], b[:], f1_first[:], ALU.subtract)
        f3_rest = sb.tile([P, T], F32, tag="b_then_f3")
        nc.gpsimd.memset(f3_rest[:], 0.0)
        bb = sb.tile([P, U], F32, tag="bb_then_aa")
        nc.vector.tensor_tensor(bb[:], bb_part[:], f1_rest[:], ALU.subtract)
        bb_picked = sb.tile([P, SLOTS], F32)
        for first in (0, HALF):
            nc.vector.tensor_copy(bb_picked[:, first : first + HALF],
                                  bb[:].indirect(entries(idx4, first, first + HALF)))
        nc.scalar.activation(f3_first[:].indirect(entries(idx3, 0, FIRST)), bb_picked[:, 0:FIRST], COPY)
        nc.scalar.activation(f3_rest[:].indirect(entries(idx3, FIRST, SLOTS)), bb_picked[:, FIRST:SLOTS], COPY)

        aa = sb.tile([P, T], F32, tag="bb_then_aa")
        nc.vector.tensor_tensor(aa[:], a[:], f2[:], ALU.max)
        ac_part = sb.tile([P, T], F32)
        nc.vector.tensor_tensor(ac_part[:], aa[:], f3_first[:], ALU.add)
        ac = sb.tile([P, T], F32)
        nc.vector.tensor_tensor(ac[:], ac_part[:], f3_rest[:], ALU.add)

        out_low = sb.tile([P, HALF], F32)
        nc.vector.tensor_copy(out_low[:], ac[:].indirect(entries(idx5, 0, HALF)))
        nc.sync.dma_start(out[:, 0:HALF], out_low[:])
        out_high = sb.tile([P, HALF], F32)
        nc.scalar.activation(out_high[:], ac[:].indirect(entries(idx5, HALF, SLOTS)), COPY)
        nc.scalar.dma_start(out[:, HALF:SLOTS], out_high[:])
